import numpy as np
import ml_dtypes


def mxq(x, axis, fmt="e4m3"):
    dtype, down = {"e4m3": (ml_dtypes.float8_e4m3fn, 7), "e5m2": (ml_dtypes.float8_e5m2, 14)}[fmt]
    v = np.moveaxis(np.asarray(x, np.float32).astype(ml_dtypes.bfloat16).astype(np.float64), axis, -1)
    blocks = v.reshape(v.shape[:-1] + (-1, 32))
    amax = np.abs(blocks).max(-1, keepdims=True)
    byte = np.maximum(np.where(amax > 0, np.frexp(amax)[1] - 1 + 127, 0) - down, 1)
    scale = np.exp2(byte - 127.0)
    codes = (blocks / scale).astype(np.float32).astype(dtype).astype(np.float64)
    return np.moveaxis((codes * scale).reshape(v.shape), -1, axis)


WIDE = False


def mx_kscale(k):
    if not WIDE:
        return np.ones(k)
    levels = np.array([10, -10, 5, -5, 0])
    if k % 512:
        return np.exp2(np.random.permutation(np.resize(levels, k // 32))).repeat(32)
    a = np.empty((k // 512, 16))
    for p in range(k // 512):
        a[p, :8] = np.random.permutation(np.resize(levels, 8))
        for g in range(8):
            far = levels[np.abs(levels - a[p, g]) >= 10]
            a[p, g + 8] = far[np.random.randint(len(far))]
    return np.exp2(a.ravel()).repeat(32)


def f64(x):
    return np.asarray(x).astype(np.float64)


def striped8(idx):
    return np.asarray(idx).reshape(8, -1, 16).transpose(0, 2, 1).reshape(128, -1).astype(np.uint16)


def unstriped8(offs):
    return offs.reshape(8, 16, -1).transpose(0, 2, 1).reshape(8, -1).astype(np.int64)


def pick8(x, idx, run):
    r = np.arange(len(x))
    return x[r[:, None], idx[r % (8 * run) // run]]


E2M1 = np.array([0.0, 0.5, 1.0, 1.5, 2.0, 3.0, 4.0, 6.0, -0.0, -0.5, -1.0, -1.5, -2.0, -3.0, -4.0, -6.0])


def pack_weight(w, fmt):
    k, n = w.shape
    w = f64(np.asarray(w, np.float32).astype(ml_dtypes.bfloat16)).reshape(k // 32, 32, n)
    amax = np.abs(w).max(1)
    if fmt == "e4m3":
        byte = np.frexp(amax)[1] - 1 + 127 - 7
    else:
        mant, ex = np.frexp(amax / 6.0)
        byte = np.where(mant > 0.5, ex, ex - 1) + 127
    byte = np.clip(np.where(amax > 0, byte, 1), 1, 254)
    scaled = (w * np.exp2(127.0 - byte)[:, None, :]).reshape(k, n).astype(np.float32)
    by_word = np.ascontiguousarray(scaled.reshape(k // 512, 128, 4, n).transpose(0, 1, 3, 2))
    if fmt == "e4m3":
        words = by_word.astype(ml_dtypes.float8_e4m3fn).view(np.uint8)
    else:
        c = by_word.astype(ml_dtypes.float4_e2m1fn).view(np.uint8) & 0xF
        words = (c[..., 0::2] | (c[..., 1::2] << 4)).reshape(k // 512, 128, 2 * n)
    return np.ascontiguousarray(words), np.ascontiguousarray(byte.astype(np.uint8).reshape(k // 512, 16, n))


def unpack_weight(words, scales, fmt):
    g, _, n = scales.shape
    words = np.ascontiguousarray(words).reshape(g, 128, n, -1)
    if fmt == "e4m3":
        vals = words.view(ml_dtypes.float8_e4m3fn).astype(np.float64)
    else:
        nib = np.empty((g, 128, n, 4), np.uint8)
        nib[..., 0::2] = words & 0xF
        nib[..., 1::2] = words >> 4
        vals = E2M1[nib]
    vals = vals * np.repeat(np.exp2(scales.astype(np.float64) - 127.0), 8, axis=1)[..., None]
    return vals.transpose(0, 1, 3, 2).reshape(g * 512, n)


def sigmoid(v):
    return 1.0 / (1.0 + np.exp(-v))


D, T, U, X, S, I, Q = 512, 1024, 1024, 1024, 1024, 512, 128


def setup_inputs():
    n = np.random.standard_normal
    idx = np.stack([np.random.permutation(T)[:I] for _ in range(8)])
    idx2 = np.stack([np.random.permutation(U)[:I] for _ in range(8)])
    idx3 = np.stack([np.random.permutation(X)[:I] for _ in range(8)])
    idx4 = np.stack([np.random.permutation(S)[:I] for _ in range(8)])
    idx5 = np.stack([np.random.permutation(T)[:I] for _ in range(8)])
    idx6 = np.stack([np.random.permutation(S)[:I] for _ in range(8)])
    fd = mx_kscale(D)
    keysp = pack_weight(n((D, T)) / fd[:, None], "e2m1")
    notesp = pack_weight(n((D, U)) / fd[:, None], "e4m3")
    usersp = pack_weight(n((D, X)) / fd[:, None], "e2m1")
    shelvesp = pack_weight(n((D, S)) / fd[:, None], "e4m3")
    return {
        "query": (n((D, Q)) * 1.0 / np.sqrt(D) * fd[:, None]).astype(np.float32),
        "keys_words": keysp[0],
        "keys_scales": keysp[1],
        "notes_words": notesp[0],
        "notes_scales": notesp[1],
        "users_words": usersp[0],
        "users_scales": usersp[1],
        "shelves_words": shelvesp[0],
        "shelves_scales": shelvesp[1],
        "thr": (np.random.uniform(-0.6, 0.6, (Q, 1))).astype(np.float32),
        "slope": (np.random.uniform(1.0, 3.0, (Q, 1))).astype(np.float32),
        "offs": striped8(idx),
        "offs2": striped8(idx2),
        "offs3": striped8(idx3),
        "offs4": striped8(idx4),
        "offs5": striped8(idx5),
        "offs6": striped8(idx6),
    }


def reference(query, keys_words, keys_scales, notes_words, notes_scales, users_words, users_scales, shelves_words, shelves_scales, thr, slope, offs, offs2, offs3, offs4, offs5, offs6):
    idx = unstriped8(offs)
    idx2 = unstriped8(offs2)
    idx3 = unstriped8(offs3)
    idx4 = unstriped8(offs4)
    idx5 = unstriped8(offs5)
    idx6 = unstriped8(offs6)
    keysu = unpack_weight(keys_words, keys_scales, "e2m1")
    notesu = unpack_weight(notes_words, notes_scales, "e4m3")
    usersu = unpack_weight(users_words, users_scales, "e2m1")
    shelvesu = unpack_weight(shelves_words, shelves_scales, "e4m3")
    queryq = mxq(f64(query), 0, "e4m3")
    a = queryq.T @ keysu
    b = queryq.T @ notesu
    c0 = queryq.T @ usersu
    d0 = queryq.T @ shelvesu
    s1 = sigmoid(pick8(d0, idx4, 16) * f64(slope) + f64(thr))
    w = np.maximum(pick8(a, idx, 16), pick8(b, idx2, 16))
    r = w - pick8(c0, idx3, 16)
    v = r * s1
    f1 = np.zeros((Q, T))
    f1[np.arange(Q)[:, None], idx[np.arange(Q) % 128 // 16]] = v
    aa = a + f1
    y = pick8(aa, idx5, 16) + pick8(d0, idx6, 16)
    return y

@@ -1,0 +1,172 @@
+from contextlib import ExitStack
+
+import concourse.mybir as mybir
+
+F32 = mybir.dt.float32
+BF16 = mybir.dt.bfloat16
+I32 = mybir.dt.int32
+U32 = mybir.dt.uint32
+U16 = mybir.dt.uint16
+U8 = mybir.dt.uint8
+FP8X4 = mybir.dt.float8_e4m3fn_x4
+FP4X4 = mybir.dt.float4_e2m1fn_x4
+ALU = mybir.AluOpType
+ACT = mybir.ActivationFunctionType
+
+P = 128
+PACK = 4
+D, POOL, SLOTS, Q = 512, 1024, 512, 128
+BANK = 512
+HALF = SLOTS // 2
+LIST_COLS = SLOTS // 16
+
+FLOPS = 2 * D * Q * 4 * POOL
+
+
+def tile_attend_openshelf_four_kernel(
+    tc, query, keys_words, keys_scales, notes_words, notes_scales, users_words, users_scales,
+    shelves_words, shelves_scales, thr, slope, offs, offs2, offs3, offs4, offs5, offs6, out,
+):
+    nc = tc.nc
+    with ExitStack() as ctx:
+        keep = ctx.enter_context(tc.tile_pool(name="keep", bufs=1))
+        psum = ctx.enter_context(tc.psum_pool(name="psum", bufs=1))
+
+        def load_list(name, src):
+            t = keep.tile([P, LIST_COLS], U16, name=name)
+            nc.sync.dma_start(t[:], src)
+            return t
+
+        def zeroed_plane(name):
+            t = keep.tile([P, POOL], U8, name=name, align_bytes=64)
+            nc.vector.memset(t[:].bitcast(I32), 0)
+            return t
+
+        def load_scales(queues, plane, src, first):
+            for quad in range(4):
+                row = 32 * quad + first
+                queues[quad].dma_start(plane[row : row + 4, :].bitcast(I32), src[0, 4 * quad : 4 * quad + 4, :].bitcast(I32))
+
+        def load_words(name, src, word_bytes):
+            t = keep.tile([P, POOL * word_bytes], U8, name=name, align_bytes=64)
+            nc.sync.dma_start(t[:].bitcast(I32), src.bitcast(I32))
+            return t
+
+        def half_list(t, h):
+            return t[:, h * LIST_COLS // 2 : (h + 1) * LIST_COLS // 2]
+
+        def half(t, h):
+            return t[:, h * HALF : (h + 1) * HALF]
+
+        d_plane = zeroed_plane("d_plane")
+        b_plane = zeroed_plane("b_plane")
+        a_plane = zeroed_plane("a_plane")
+        c_plane = zeroed_plane("c_plane")
+
+        q_raw = keep.tile([P, PACK, Q], F32, name="q_raw")
+        nc.sync.dma_start(q_raw[:], query.rearrange("(p j) w -> p j w", j=PACK))
+        load_scales((nc.scalar, nc.sync, nc.scalar, nc.sync), d_plane, shelves_scales, 8)
+        d_words = load_words("d_words", shelves_words[0].rearrange("p n t -> p (n t)"), 4)
+        b_words = load_words("b_words", notes_words[0].rearrange("p n t -> p (n t)"), 4)
+        l4 = load_list("l4", offs4)
+        slope_t = keep.tile([P, 1], F32, name="slope_t")
+        nc.gpsimd.dma_start(slope_t[:], slope)
+        thr_t = keep.tile([P, 1], F32, name="thr_t")
+        nc.gpsimd.dma_start(thr_t[:], thr)
+        load_scales((nc.scalar,) * 4, b_plane, notes_scales, 4)
+        a_words = load_words("a_words", keys_words[0], 2)
+        load_scales((nc.scalar, nc.scalar, nc.scalar, nc.gpsimd), a_plane, keys_scales, 0)
+        c_words = load_words("c_words", users_words[0], 2)
+        l2 = load_list("l2", offs2)
+        load_scales((nc.sync, nc.sync, nc.gpsimd, nc.gpsimd), c_plane, users_scales, 0)
+        l1 = load_list("l1", offs)
+        l3 = load_list("l3", offs3)
+        l6 = load_list("l6", offs6)
+        l5 = load_list("l5", offs5)
+
+        q_bf = keep.tile([P, Q, PACK], BF16, name="q_bf", align_bytes=64)
+        nc.vector.tensor_copy(q_bf[:], q_raw[:].rearrange("p j w -> p w j"))
+        q_codes = keep.tile([P, Q], U32, name="q_codes", align_bytes=64)
+        q_plane = keep.tile([P, Q], U8, name="q_plane", align_bytes=64)
+        nc.vector.quantize_mx(q_codes[:].bitcast(FP8X4), q_plane[:], q_bf[:].rearrange("p w j -> p (w j)"))
+
+        f1 = keep.tile([P, POOL], F32, name="f1")
+        nc.gpsimd.memset(f1[:], 0.0)
+
+        def scores(name, words, plane, first, fmt, word_bytes):
+            banks = []
+            for n in range(POOL // BANK):
+                bank = psum.tile([P, BANK], F32, name=name + "_bank%d" % n)
+                nc.tensor.matmul_mx(
+                    bank[:],
+                    lhsT=q_codes[:].bitcast(FP8X4),
+                    lhsT_scale=q_plane[:],
+                    rhs=words[:, n * BANK * word_bytes : (n + 1) * BANK * word_bytes].bitcast(fmt),
+                    rhs_scale=plane[first:P, n * BANK : (n + 1) * BANK],
+                    start=True,
+                    stop=True,
+                )
+                banks.append(bank)
+            return banks
+
+        d_banks = scores("d", d_words, d_plane, 8, FP8X4, 4)
+        b_banks = scores("b", b_words, b_plane, 4, FP8X4, 4)
+        a_banks = scores("a", a_words, a_plane, 0, FP4X4, 2)
+        c_banks = scores("c", c_words, c_plane, 0, FP4X4, 2)
+
+        d0 = keep.tile([P, POOL], F32, name="d0")
+        b = keep.tile([P, POOL], F32, name="b")
+        a = keep.tile([P, POOL], F32, name="a")
+        c0 = keep.tile([P, POOL], F32, name="c0")
+        ga = keep.tile([P, SLOTS], F32, name="ga")
+        gb = keep.tile([P, SLOTS], F32, name="gb", tag="gb")
+        gc = keep.tile([P, SLOTS], F32, name="gc")
+        gd = keep.tile([P, SLOTS], F32, name="gd")
+        w = keep.tile([P, SLOTS], F32, name="w")
+        aa = keep.tile([P, POOL], F32, name="aa")
+        g5 = keep.tile([P, HALF], F32, name="g5")
+        y = keep.tile([P, SLOTS], F32, name="y")
+
+        def v_out(dst, banks, n):
+            nc.vector.tensor_copy(dst[:, n * BANK : (n + 1) * BANK], banks[n][:])
+
+        def s_out(dst, banks, n):
+            nc.scalar.copy(dst[:, n * BANK : (n + 1) * BANK], banks[n][:])
+
+        def s_gather(dst, table, lst, h):
+            nc.scalar.activation(dst, table[:].indirect(half_list(lst, h)), ACT.Copy)
+
+        def gate(h, tag):
+            s1 = keep.tile([P, HALF], F32, name="s1_%d" % h, tag=tag)
+            nc.scalar.activation(s1[:], d0[:].indirect(half_list(l4, h)), ACT.Sigmoid, bias=thr_t[:], scale=slope_t[:])
+            return s1
+
+        def put(h, s1):
+            r = keep.tile([P, HALF], F32, name="r_%d" % h, tag="r")
+            nc.vector.tensor_tensor(r[:], half(w, h), half(gc, h), ALU.subtract)
+            nc.vector.tensor_tensor(f1[:].indirect(half_list(l1, h)), r[:], s1[:], ALU.mult)
+
+        v_out(d0, d_banks, 0)
+        v_out(d0, d_banks, 1)
+        s1 = gate(0, "s1_first")
+        v_out(b, b_banks, 0)
+        v_out(b, b_banks, 1)
+        s_out(a, a_banks, 0)
+        s_out(a, a_banks, 1)
+        nc.vector.tensor_copy(gb[:], b[:].indirect(l2[:]))
+        s_out(c0, c_banks, 0)
+        s_out(c0, c_banks, 1)
+        nc.vector.tensor_copy(ga[:], a[:].indirect(l1[:]))
+        nc.vector.tensor_tensor(w[:], ga[:], gb[:], ALU.max)
+        s_gather(half(gc, 0), c0, l3, 0)
+        put(0, s1)
+        s_gather(half(gc, 1), c0, l3, 1)
+        s1 = gate(1, "gb")
+        put(1, s1)
+        nc.scalar.activation(gd[:], d0[:].indirect(l6[:]), ACT.Copy)
+        nc.vector.tensor_tensor(aa[:], a[:], f1[:], ALU.add)
+        nc.vector.tensor_tensor(half(y, 0), aa[:].indirect(half_list(l5, 0)), half(gd, 0), ALU.add)
+        s_gather(g5[:], aa, l5, 1)
+        nc.sync.dma_start(half(out, 0), half(y, 0))
+        nc.vector.tensor_tensor(half(y, 1), g5[:], half(gd, 1), ALU.add)
+        nc.sync.dma_start(half(out, 1), half(y, 1))

@@ -37,16 +37,6 @@ def tile_attend_openshelf_four_kernel(
             nc.sync.dma_start(t[:], src)
             return t
 
-        def zeroed_plane(name):
-            t = keep.tile([P, POOL], U8, name=name, align_bytes=64)
-            nc.vector.memset(t[:].bitcast(I32), 0)
-            return t
-
-        def load_scales(queues, plane, src, first):
-            for quad in range(4):
-                row = 32 * quad + first
-                queues[quad].dma_start(plane[row : row + 4, :].bitcast(I32), src[0, 4 * quad : 4 * quad + 4, :].bitcast(I32))
-
         def load_words(name, src, word_bytes):
             t = keep.tile([P, POOL * word_bytes], U8, name=name, align_bytes=64)
             nc.sync.dma_start(t[:].bitcast(I32), src.bitcast(I32))
@@ -58,29 +48,48 @@ def tile_attend_openshelf_four_kernel(
         def half(t, h):
             return t[:, h * HALF : (h + 1) * HALF]
 
-        d_plane = zeroed_plane("d_plane")
-        b_plane = zeroed_plane("b_plane")
-        a_plane = zeroed_plane("a_plane")
-        c_plane = zeroed_plane("c_plane")
+        a_plane = keep.tile([P, POOL], U8, name="a_plane", align_bytes=64)
+        nc.vector.memset(a_plane[:].bitcast(I32), 0)
+        warm_in = keep.tile([P, 1], F32, name="warm_in")
+        nc.vector.memset(warm_in[:], 0.0)
+        planes = keep.tile([P, 2 * POOL], U8, name="planes", align_bytes=64)
+        nc.vector.memset(planes[:].bitcast(I32), 0)
+        c_plane, b_plane = (planes[:, n * POOL : (n + 1) * POOL] for n in range(2))
+        d_plane = keep.tile([P, POOL], U8, name="d_plane", align_bytes=64)
+        nc.vector.memset(d_plane[:].bitcast(I32), 0)
 
+        queues = (nc.sync, nc.scalar)
+        stage = keep.tile([32, 2 * POOL], U8, name="stage")
+        for n, src in enumerate((users_scales, notes_scales)):
+            queues[n].dma_start(stage[16:32, n * POOL : (n + 1) * POOL].bitcast(I32), src[0].bitcast(I32))
         q_raw = keep.tile([P, PACK, Q], F32, name="q_raw")
         nc.sync.dma_start(q_raw[:], query.rearrange("(p j) w -> p j w", j=PACK))
-        load_scales((nc.scalar, nc.sync, nc.scalar, nc.sync), d_plane, shelves_scales, 8)
-        d_words = load_words("d_words", shelves_words[0].rearrange("p n t -> p (n t)"), 4)
-        b_words = load_words("b_words", notes_words[0].rearrange("p n t -> p (n t)"), 4)
-        l4 = load_list("l4", offs4)
+        for quad, queue in enumerate((nc.scalar, nc.sync, nc.scalar, nc.scalar)):
+            queue.dma_start(
+                a_plane[32 * quad : 32 * quad + 4, :].bitcast(I32), keys_scales[0, 4 * quad : 4 * quad + 4, :].bitcast(I32)
+            )
+        a_words = load_words("a_words", keys_words[0], 2)
+        warm_out = keep.tile([P, 1], F32, name="warm_out")
+        nc.scalar.activation(warm_out[:], warm_in[:], ACT.Sigmoid)
         slope_t = keep.tile([P, 1], F32, name="slope_t")
         nc.gpsimd.dma_start(slope_t[:], slope)
         thr_t = keep.tile([P, 1], F32, name="thr_t")
         nc.gpsimd.dma_start(thr_t[:], thr)
-        load_scales((nc.scalar,) * 4, b_plane, notes_scales, 4)
-        a_words = load_words("a_words", keys_words[0], 2)
-        load_scales((nc.scalar, nc.scalar, nc.scalar, nc.gpsimd), a_plane, keys_scales, 0)
         c_words = load_words("c_words", users_words[0], 2)
-        l2 = load_list("l2", offs2)
-        load_scales((nc.sync, nc.sync, nc.gpsimd, nc.gpsimd), c_plane, users_scales, 0)
+        for quad in range(4):
+            nc.sync.dma_start(
+                planes[32 * quad : 32 * quad + 4, :].bitcast(I32), stage[16 + 4 * quad : 20 + 4 * quad, :].bitcast(I32)
+            )
         l1 = load_list("l1", offs)
         l3 = load_list("l3", offs3)
+        b_words = load_words("b_words", notes_words[0].rearrange("p n t -> p (n t)"), 4)
+        d_words = load_words("d_words", shelves_words[0].rearrange("p n t -> p (n t)"), 4)
+        for quad in range(4):
+            nc.sync.dma_start(
+                d_plane[32 * quad + 8 : 32 * quad + 12, :].bitcast(I32), shelves_scales[0, 4 * quad : 4 * quad + 4, :].bitcast(I32)
+            )
+        l2 = load_list("l2", offs2)
+        l4 = load_list("l4", offs4)
         l6 = load_list("l6", offs6)
         l5 = load_list("l5", offs5)
 
@@ -109,20 +118,21 @@ def tile_attend_openshelf_four_kernel(
                 banks.append(bank)
             return banks
 
-        d_banks = scores("d", d_words, d_plane, 8, FP8X4, 4)
-        b_banks = scores("b", b_words, b_plane, 4, FP8X4, 4)
         a_banks = scores("a", a_words, a_plane, 0, FP4X4, 2)
         c_banks = scores("c", c_words, c_plane, 0, FP4X4, 2)
+        b_banks = scores("b", b_words, b_plane, 0, FP8X4, 4)
+        d_banks = scores("d", d_words, d_plane, 8, FP8X4, 4)
 
         d0 = keep.tile([P, POOL], F32, name="d0")
         b = keep.tile([P, POOL], F32, name="b")
         a = keep.tile([P, POOL], F32, name="a")
         c0 = keep.tile([P, POOL], F32, name="c0")
-        ga = keep.tile([P, SLOTS], F32, name="ga")
-        gb = keep.tile([P, SLOTS], F32, name="gb", tag="gb")
+        ga = keep.tile([P, SLOTS], F32, name="ga", tag="ga")
         gc = keep.tile([P, SLOTS], F32, name="gc")
+        gb = keep.tile([P, SLOTS], F32, name="gb")
         gd = keep.tile([P, SLOTS], F32, name="gd")
         w = keep.tile([P, SLOTS], F32, name="w")
+        r = keep.tile([P, SLOTS], F32, name="r")
         aa = keep.tile([P, POOL], F32, name="aa")
         g5 = keep.tile([P, HALF], F32, name="g5")
         y = keep.tile([P, SLOTS], F32, name="y")
@@ -136,33 +146,33 @@ def tile_attend_openshelf_four_kernel(
         def s_gather(dst, table, lst, h):
             nc.scalar.activation(dst, table[:].indirect(half_list(lst, h)), ACT.Copy)
 
-        def gate(h, tag):
-            s1 = keep.tile([P, HALF], F32, name="s1_%d" % h, tag=tag)
+        def v_gather(dst, table, lst, h):
+            nc.vector.tensor_copy(dst, table[:].indirect(half_list(lst, h)))
+
+        def gate(h):
+            s1 = keep.tile([P, HALF], F32, name="s1_%d" % h)
             nc.scalar.activation(s1[:], d0[:].indirect(half_list(l4, h)), ACT.Sigmoid, bias=thr_t[:], scale=slope_t[:])
             return s1
 
-        def put(h, s1):
-            r = keep.tile([P, HALF], F32, name="r_%d" % h, tag="r")
-            nc.vector.tensor_tensor(r[:], half(w, h), half(gc, h), ALU.subtract)
-            nc.vector.tensor_tensor(f1[:].indirect(half_list(l1, h)), r[:], s1[:], ALU.mult)
-
-        v_out(d0, d_banks, 0)
-        v_out(d0, d_banks, 1)
-        s1 = gate(0, "s1_first")
-        v_out(b, b_banks, 0)
-        v_out(b, b_banks, 1)
         s_out(a, a_banks, 0)
-        s_out(a, a_banks, 1)
-        nc.vector.tensor_copy(gb[:], b[:].indirect(l2[:]))
+        v_out(a, a_banks, 1)
+        nc.vector.tensor_copy(ga[:], a[:].indirect(l1[:]))
         s_out(c0, c_banks, 0)
         s_out(c0, c_banks, 1)
-        nc.vector.tensor_copy(ga[:], a[:].indirect(l1[:]))
-        nc.vector.tensor_tensor(w[:], ga[:], gb[:], ALU.max)
-        s_gather(half(gc, 0), c0, l3, 0)
-        put(0, s1)
-        s_gather(half(gc, 1), c0, l3, 1)
-        s1 = gate(1, "gb")
-        put(1, s1)
+        nc.vector.tensor_copy(gc[:], c0[:].indirect(l3[:]))
+        s_out(b, b_banks, 0)
+        s_out(b, b_banks, 1)
+        s_out(d0, d_banks, 0)
+        v_out(d0, d_banks, 1)
+        s_gather(half(gb, 0), b, l2, 0)
+        v_gather(half(gb, 1), b, l2, 1)
+        s1 = [gate(h) for h in range(2)]
+        for h in range(2):
+            nc.vector.tensor_tensor(half(w, h), half(ga, h), half(gb, h), ALU.max)
+        for h in range(2):
+            nc.vector.tensor_tensor(half(r, h), half(w, h), half(gc, h), ALU.subtract)
+        for h in range(2):
+            nc.vector.tensor_tensor(f1[:].indirect(half_list(l1, h)), half(r, h), s1[h][:], ALU.mult)
         nc.scalar.activation(gd[:], d0[:].indirect(l6[:]), ACT.Copy)
         nc.vector.tensor_tensor(aa[:], a[:], f1[:], ALU.add)
         nc.vector.tensor_tensor(half(y, 0), aa[:].indirect(half_list(l5, 0)), half(gd, 0), ALU.add)

@@ -48,48 +48,36 @@ def tile_attend_openshelf_four_kernel(
         def half(t, h):
             return t[:, h * HALF : (h + 1) * HALF]
 
-        a_plane = keep.tile([P, POOL], U8, name="a_plane", align_bytes=64)
-        nc.vector.memset(a_plane[:].bitcast(I32), 0)
-        warm_in = keep.tile([P, 1], F32, name="warm_in")
-        nc.vector.memset(warm_in[:], 0.0)
-        planes = keep.tile([P, 2 * POOL], U8, name="planes", align_bytes=64)
-        nc.vector.memset(planes[:].bitcast(I32), 0)
-        c_plane, b_plane = (planes[:, n * POOL : (n + 1) * POOL] for n in range(2))
-        d_plane = keep.tile([P, POOL], U8, name="d_plane", align_bytes=64)
-        nc.vector.memset(d_plane[:].bitcast(I32), 0)
-
+        stage = keep.tile([P, 2 * POOL], U8, name="stage")
         queues = (nc.sync, nc.scalar)
-        stage = keep.tile([32, 2 * POOL], U8, name="stage")
-        for n, src in enumerate((users_scales, notes_scales)):
-            queues[n].dma_start(stage[16:32, n * POOL : (n + 1) * POOL].bitcast(I32), src[0].bitcast(I32))
+        for group, pair in enumerate(((keys_scales, notes_scales), (users_scales, shelves_scales))):
+            for u, src in enumerate(pair):
+                queues[u].dma_start(stage[3 * u : 96 : 6, group * POOL : (group + 1) * POOL].bitcast(I32), src[0].bitcast(I32))
+        nc.vector.memset(stage[96:P, :].bitcast(I32), 0)
+        f1 = keep.tile([P, POOL], F32, name="f1")
+        nc.vector.memset(f1[:], 0.0)
+
         q_raw = keep.tile([P, PACK, Q], F32, name="q_raw")
         nc.sync.dma_start(q_raw[:], query.rearrange("(p j) w -> p j w", j=PACK))
-        for quad, queue in enumerate((nc.scalar, nc.sync, nc.scalar, nc.scalar)):
-            queue.dma_start(
-                a_plane[32 * quad : 32 * quad + 4, :].bitcast(I32), keys_scales[0, 4 * quad : 4 * quad + 4, :].bitcast(I32)
-            )
         a_words = load_words("a_words", keys_words[0], 2)
-        warm_out = keep.tile([P, 1], F32, name="warm_out")
-        nc.scalar.activation(warm_out[:], warm_in[:], ACT.Sigmoid)
-        slope_t = keep.tile([P, 1], F32, name="slope_t")
-        nc.gpsimd.dma_start(slope_t[:], slope)
-        thr_t = keep.tile([P, 1], F32, name="thr_t")
-        nc.gpsimd.dma_start(thr_t[:], thr)
         c_words = load_words("c_words", users_words[0], 2)
-        for quad in range(4):
-            nc.sync.dma_start(
-                planes[32 * quad : 32 * quad + 4, :].bitcast(I32), stage[16 + 4 * quad : 20 + 4 * quad, :].bitcast(I32)
-            )
         l1 = load_list("l1", offs)
-        l3 = load_list("l3", offs3)
+        planes = keep.tile([P, 2 * POOL], U8, name="planes", align_bytes=64)
+        for row in range(4):
+            queues[1 - row % 2].dma_start(planes[row:P:4, :].bitcast(I32), stage[6 * row : 6 * row + 96 : 3, :].bitcast(I32))
+        warm_out = keep.tile([P, 1], F32, name="warm_out")
+        nc.scalar.activation(warm_out[:], q_raw[:, 0, 0:1], ACT.Sigmoid)
+        a_plane = b_plane = planes[:, 0:POOL]
+        c_plane = d_plane = planes[:, POOL : 2 * POOL]
         b_words = load_words("b_words", notes_words[0].rearrange("p n t -> p (n t)"), 4)
         d_words = load_words("d_words", shelves_words[0].rearrange("p n t -> p (n t)"), 4)
-        for quad in range(4):
-            nc.sync.dma_start(
-                d_plane[32 * quad + 8 : 32 * quad + 12, :].bitcast(I32), shelves_scales[0, 4 * quad : 4 * quad + 4, :].bitcast(I32)
-            )
-        l2 = load_list("l2", offs2)
+        l3 = load_list("l3", offs3)
         l4 = load_list("l4", offs4)
+        slope_t = keep.tile([P, 1], F32, name="slope_t")
+        nc.sync.dma_start(slope_t[:], slope)
+        l2 = load_list("l2", offs2)
+        thr_t = keep.tile([P, 1], F32, name="thr_t")
+        nc.sync.dma_start(thr_t[:], thr)
         l6 = load_list("l6", offs6)
         l5 = load_list("l5", offs5)
 
@@ -99,8 +87,6 @@ def tile_attend_openshelf_four_kernel(
         q_plane = keep.tile([P, Q], U8, name="q_plane", align_bytes=64)
         nc.vector.quantize_mx(q_codes[:].bitcast(FP8X4), q_plane[:], q_bf[:].rearrange("p w j -> p (w j)"))
 
-        f1 = keep.tile([P, POOL], F32, name="f1")
-        nc.gpsimd.memset(f1[:], 0.0)
 
         def scores(name, words, plane, first, fmt, word_bytes):
             banks = []
@@ -120,18 +106,15 @@ def tile_attend_openshelf_four_kernel(
 
         a_banks = scores("a", a_words, a_plane, 0, FP4X4, 2)
         c_banks = scores("c", c_words, c_plane, 0, FP4X4, 2)
-        b_banks = scores("b", b_words, b_plane, 0, FP8X4, 4)
-        d_banks = scores("d", d_words, d_plane, 8, FP8X4, 4)
+        b_banks = scores("b", b_words, b_plane, 4, FP8X4, 4)
+        d_banks = scores("d", d_words, d_plane, 4, FP8X4, 4)
 
         d0 = keep.tile([P, POOL], F32, name="d0")
         b = keep.tile([P, POOL], F32, name="b")
         a = keep.tile([P, POOL], F32, name="a")
         c0 = keep.tile([P, POOL], F32, name="c0")
         ga = keep.tile([P, SLOTS], F32, name="ga", tag="ga")
-        gc = keep.tile([P, SLOTS], F32, name="gc")
         gb = keep.tile([P, SLOTS], F32, name="gb")
-        gd = keep.tile([P, SLOTS], F32, name="gd")
-        w = keep.tile([P, SLOTS], F32, name="w")
         r = keep.tile([P, SLOTS], F32, name="r")
         aa = keep.tile([P, POOL], F32, name="aa")
         g5 = keep.tile([P, HALF], F32, name="g5")
@@ -154,25 +137,35 @@ def tile_attend_openshelf_four_kernel(
             nc.scalar.activation(s1[:], d0[:].indirect(half_list(l4, h)), ACT.Sigmoid, bias=thr_t[:], scale=slope_t[:])
             return s1
 
+        def larger(h):
+            w = keep.tile([P, HALF], F32, name="w_%d" % h, tag="w_%d" % h)
+            nc.vector.tensor_tensor(w[:], half(ga, h), half(gb, h), ALU.max)
+            return w
+
+        def put(h, s1, w, gc):
+            nc.vector.tensor_tensor(half(r, h), w[:], gc[:], ALU.subtract)
+            nc.vector.tensor_tensor(f1[:].indirect(half_list(l1, h)), half(r, h), s1[:], ALU.mult)
+
         s_out(a, a_banks, 0)
         v_out(a, a_banks, 1)
         nc.vector.tensor_copy(ga[:], a[:].indirect(l1[:]))
         s_out(c0, c_banks, 0)
         s_out(c0, c_banks, 1)
-        nc.vector.tensor_copy(gc[:], c0[:].indirect(l3[:]))
         s_out(b, b_banks, 0)
-        s_out(b, b_banks, 1)
+        v_out(b, b_banks, 1)
+        gc = keep.tile([P, HALF], F32, name="gc_0", tag="gc")
+        v_gather(gc[:], c0, l3, 0)
+        v_gather(half(gb, 0), b, l2, 0)
         s_out(d0, d_banks, 0)
-        v_out(d0, d_banks, 1)
-        s_gather(half(gb, 0), b, l2, 0)
-        v_gather(half(gb, 1), b, l2, 1)
+        s_out(d0, d_banks, 1)
+        s_gather(half(gb, 1), b, l2, 1)
         s1 = [gate(h) for h in range(2)]
-        for h in range(2):
-            nc.vector.tensor_tensor(half(w, h), half(ga, h), half(gb, h), ALU.max)
-        for h in range(2):
-            nc.vector.tensor_tensor(half(r, h), half(w, h), half(gc, h), ALU.subtract)
-        for h in range(2):
-            nc.vector.tensor_tensor(f1[:].indirect(half_list(l1, h)), half(r, h), s1[h][:], ALU.mult)
+        w = [larger(h) for h in range(2)]
+        put(0, s1[0], w[0], gc)
+        gc = keep.tile([P, HALF], F32, name="gc_1", tag="gc")
+        s_gather(gc[:], c0, l3, 1)
+        put(1, s1[1], w[1], gc)
+        gd = keep.tile([P, SLOTS], F32, name="gd", tag="w_0")
         nc.scalar.activation(gd[:], d0[:].indirect(l6[:]), ACT.Copy)
         nc.vector.tensor_tensor(aa[:], a[:], f1[:], ALU.add)
         nc.vector.tensor_tensor(half(y, 0), aa[:].indirect(half_list(l5, 0)), half(gd, 0), ALU.add)

@@ -167,7 +167,10 @@ def tile_attend_openshelf_four_kernel(
         put(1, s1[1], w[1], gc)
         gd = keep.tile([P, SLOTS], F32, name="gd", tag="w_0")
         nc.scalar.activation(gd[:], d0[:].indirect(l6[:]), ACT.Copy)
-        nc.vector.tensor_tensor(aa[:], a[:], f1[:], ALU.add)
+        cut = POOL - 224
+        nc.gpsimd.tensor_tensor(aa[:, cut:POOL], a[:, cut:POOL], f1[:, cut:POOL], ALU.add)
+        nc.vector.tensor_tensor(aa[:, 0:BANK], a_banks[0][:], f1[:, 0:BANK], ALU.add)
+        nc.vector.tensor_tensor(aa[:, BANK:cut], a_banks[1][:, 0 : cut - BANK], f1[:, BANK:cut], ALU.add)
         nc.vector.tensor_tensor(half(y, 0), aa[:].indirect(half_list(l5, 0)), half(gd, 0), ALU.add)
         s_gather(g5[:], aa, l5, 1)
         nc.sync.dma_start(half(out, 0), half(y, 0))

from contextlib import ExitStack

import concourse.mybir as mybir

F32 = mybir.dt.float32
BF16 = mybir.dt.bfloat16
I32 = mybir.dt.int32
U32 = mybir.dt.uint32
U16 = mybir.dt.uint16
U8 = mybir.dt.uint8
FP8X4 = mybir.dt.float8_e4m3fn_x4
FP4X4 = mybir.dt.float4_e2m1fn_x4
ALU = mybir.AluOpType
ACT = mybir.ActivationFunctionType

P = 128
PACK = 4
D, POOL, SLOTS, Q = 512, 1024, 512, 128
BANK = 512
HALF = SLOTS // 2
LIST_COLS = SLOTS // 16

FLOPS = 2 * D * Q * 4 * POOL


def tile_attend_openshelf_four_kernel(
    tc, query, keys_words, keys_scales, notes_words, notes_scales, users_words, users_scales,
    shelves_words, shelves_scales, thr, slope, offs, offs2, offs3, offs4, offs5, offs6, out,
):
    nc = tc.nc
    with ExitStack() as ctx:
        keep = ctx.enter_context(tc.tile_pool(name="keep", bufs=1))
        psum = ctx.enter_context(tc.psum_pool(name="psum", bufs=1))

        def load_list(name, src):
            t = keep.tile([P, LIST_COLS], U16, name=name)
            nc.sync.dma_start(t[:], src)
            return t

        def load_words(name, src, word_bytes):
            t = keep.tile([P, POOL * word_bytes], U8, name=name, align_bytes=64)
            nc.sync.dma_start(t[:].bitcast(I32), src.bitcast(I32))
            return t

        def half_list(t, h):
            return t[:, h * LIST_COLS // 2 : (h + 1) * LIST_COLS // 2]

        def half(t, h):
            return t[:, h * HALF : (h + 1) * HALF]

        stage = keep.tile([P, 2 * POOL], U8, name="stage")
        queues = (nc.sync, nc.scalar)
        for group, pair in enumerate(((keys_scales, notes_scales), (users_scales, shelves_scales))):
            for u, src in enumerate(pair):
                queues[u].dma_start(stage[3 * u : 96 : 6, group * POOL : (group + 1) * POOL].bitcast(I32), src[0].bitcast(I32))
        nc.vector.memset(stage[96:P, :].bitcast(I32), 0)
        f1 = keep.tile([P, POOL], F32, name="f1")
        nc.vector.memset(f1[:], 0.0)

        q_raw = keep.tile([P, PACK, Q], F32, name="q_raw")
        nc.sync.dma_start(q_raw[:], query.rearrange("(p j) w -> p j w", j=PACK))
        a_words = load_words("a_words", keys_words[0], 2)
        c_words = load_words("c_words", users_words[0], 2)
        l1 = load_list("l1", offs)
        planes = keep.tile([P, 2 * POOL], U8, name="planes", align_bytes=64)
        for row in range(4):
            queues[1 - row % 2].dma_start(planes[row:P:4, :].bitcast(I32), stage[6 * row : 6 * row + 96 : 3, :].bitcast(I32))
        warm_out = keep.tile([P, 1], F32, name="warm_out")
        nc.scalar.activation(warm_out[:], q_raw[:, 0, 0:1], ACT.Sigmoid)
        a_plane = b_plane = planes[:, 0:POOL]
        c_plane = d_plane = planes[:, POOL : 2 * POOL]
        b_words = load_words("b_words", notes_words[0].rearrange("p n t -> p (n t)"), 4)
        d_words = load_words("d_words", shelves_words[0].rearrange("p n t -> p (n t)"), 4)
        l3 = load_list("l3", offs3)
        l4 = load_list("l4", offs4)
        slope_t = keep.tile([P, 1], F32, name="slope_t")
        nc.sync.dma_start(slope_t[:], slope)
        l2 = load_list("l2", offs2)
        thr_t = keep.tile([P, 1], F32, name="thr_t")
        nc.sync.dma_start(thr_t[:], thr)
        l6 = load_list("l6", offs6)
        l5 = load_list("l5", offs5)

        q_bf = keep.tile([P, Q, PACK], BF16, name="q_bf", align_bytes=64)
        nc.vector.tensor_copy(q_bf[:], q_raw[:].rearrange("p j w -> p w j"))
        q_codes = keep.tile([P, Q], U32, name="q_codes", align_bytes=64)
        q_plane = keep.tile([P, Q], U8, name="q_plane", align_bytes=64)
        nc.vector.quantize_mx(q_codes[:].bitcast(FP8X4), q_plane[:], q_bf[:].rearrange("p w j -> p (w j)"))


        def scores(name, words, plane, first, fmt, word_bytes):
            banks = []
            for n in range(POOL // BANK):
                bank = psum.tile([P, BANK], F32, name=name + "_bank%d" % n)
                nc.tensor.matmul_mx(
                    bank[:],
                    lhsT=q_codes[:].bitcast(FP8X4),
                    lhsT_scale=q_plane[:],
                    rhs=words[:, n * BANK * word_bytes : (n + 1) * BANK * word_bytes].bitcast(fmt),
                    rhs_scale=plane[first:P, n * BANK : (n + 1) * BANK],
                    start=True,
                    stop=True,
                )
                banks.append(bank)
            return banks

        a_banks = scores("a", a_words, a_plane, 0, FP4X4, 2)
        c_banks = scores("c", c_words, c_plane, 0, FP4X4, 2)
        b_banks = scores("b", b_words, b_plane, 4, FP8X4, 4)
        d_banks = scores("d", d_words, d_plane, 4, FP8X4, 4)

        d0 = keep.tile([P, POOL], F32, name="d0")
        b = keep.tile([P, POOL], F32, name="b")
        a = keep.tile([P, POOL], F32, name="a")
        c0 = keep.tile([P, POOL], F32, name="c0")
        ga = keep.tile([P, SLOTS], F32, name="ga", tag="ga")
        gb = keep.tile([P, SLOTS], F32, name="gb")
        r = keep.tile([P, SLOTS], F32, name="r")
        aa = keep.tile([P, POOL], F32, name="aa")
        g5 = keep.tile([P, HALF], F32, name="g5")
        y = keep.tile([P, SLOTS], F32, name="y")

        def v_out(dst, banks, n):
            nc.vector.tensor_copy(dst[:, n * BANK : (n + 1) * BANK], banks[n][:])

        def s_out(dst, banks, n):
            nc.scalar.copy(dst[:, n * BANK : (n + 1) * BANK], banks[n][:])

        def s_gather(dst, table, lst, h):
            nc.scalar.activation(dst, table[:].indirect(half_list(lst, h)), ACT.Copy)

        def v_gather(dst, table, lst, h):
            nc.vector.tensor_copy(dst, table[:].indirect(half_list(lst, h)))

        def gate(h):
            s1 = keep.tile([P, HALF], F32, name="s1_%d" % h)
            nc.scalar.activation(s1[:], d0[:].indirect(half_list(l4, h)), ACT.Sigmoid, bias=thr_t[:], scale=slope_t[:])
            return s1

        def larger(h):
            w = keep.tile([P, HALF], F32, name="w_%d" % h, tag="w_%d" % h)
            nc.vector.tensor_tensor(w[:], half(ga, h), half(gb, h), ALU.max)
            return w

        def put(h, s1, w, gc):
            nc.vector.tensor_tensor(half(r, h), w[:], gc[:], ALU.subtract)
            nc.vector.tensor_tensor(f1[:].indirect(half_list(l1, h)), half(r, h), s1[:], ALU.mult)

        s_out(a, a_banks, 0)
        v_out(a, a_banks, 1)
        nc.vector.tensor_copy(ga[:], a[:].indirect(l1[:]))
        s_out(c0, c_banks, 0)
        s_out(c0, c_banks, 1)
        s_out(b, b_banks, 0)
        v_out(b, b_banks, 1)
        gc = keep.tile([P, HALF], F32, name="gc_0", tag="gc")
        v_gather(gc[:], c0, l3, 0)
        v_gather(half(gb, 0), b, l2, 0)
        s_out(d0, d_banks, 0)
        s_out(d0, d_banks, 1)
        s_gather(half(gb, 1), b, l2, 1)
        s1 = [gate(h) for h in range(2)]
        w = [larger(h) for h in range(2)]
        put(0, s1[0], w[0], gc)
        gc = keep.tile([P, HALF], F32, name="gc_1", tag="gc")
        s_gather(gc[:], c0, l3, 1)
        put(1, s1[1], w[1], gc)
        gd = keep.tile([P, SLOTS], F32, name="gd", tag="w_0")
        nc.scalar.activation(gd[:], d0[:].indirect(l6[:]), ACT.Copy)
        cut = POOL - 224
        nc.gpsimd.tensor_tensor(aa[:, cut:POOL], a[:, cut:POOL], f1[:, cut:POOL], ALU.add)
        nc.vector.tensor_tensor(aa[:, 0:BANK], a_banks[0][:], f1[:, 0:BANK], ALU.add)
        nc.vector.tensor_tensor(aa[:, BANK:cut], a_banks[1][:, 0 : cut - BANK], f1[:, BANK:cut], ALU.add)
        nc.vector.tensor_tensor(half(y, 0), aa[:].indirect(half_list(l5, 0)), half(gd, 0), ALU.add)
        s_gather(g5[:], aa, l5, 1)
        nc.sync.dma_start(half(out, 0), half(y, 0))
        nc.vector.tensor_tensor(half(y, 1), g5[:], half(gd, 1), ALU.add)
        nc.sync.dma_start(half(out, 1), half(y, 1))
